import numpy as np, ml_dtypes
CORES = [3,7,11,15,131,135,139,143]
N = 8
BF = ml_dtypes.bfloat16
W, WX, I, B, SH = 2048, 1792, 224, 8, 11
DR, IR, GAP, RO = 6, 12, 4, 4
def parts(rng):
    mid = rng.choice(np.array([0.02, 0.05, 0.15, 0.4]), (N, 8, 1, 1)); e = rng.integers(0, 16, (N, 8, 16, WX)); small = (e * 5) >> 4
    x = np.where(rng.random((N, 8, 1, WX)) < mid, e, np.where(rng.random((N, 8, 1, WX)) < 0.5, small, 11 + small))
    g = np.minimum(np.maximum(rng.integers(1, 10, (N, 8, 1, I)) + rng.integers(-2, 3, (N, 8, 16, I)), 0), 15)
    g = np.where(rng.random((N, 8, 1, I)) < 0.1, rng.integers(0, 16, g.shape), g)
    return x, g, rng.integers(0, W * WX, (N, 8, 16, W)), rng.integers(0, W, (N, 8, 16, I)), rng.integers(0, WX, (N, 8, 16, I))
def pack(x, g, rel, nam, grd):
    return {"xc": np.ascontiguousarray(x.reshape(N, 128, WX)).astype(np.float32).astype(BF), "rel": np.ascontiguousarray(rel.reshape(N, 128, W)).astype(np.int32),
            "nam": np.ascontiguousarray(nam.reshape(N, 128, I)).astype(np.int32), "grd": np.ascontiguousarray(grd.reshape(N, 128, I)).astype(np.int32),
            "lim": np.ascontiguousarray(g.reshape(N, 128, I)).astype(np.float32).astype(BF)}
def setup_inputs(rng):
    return pack(*parts(rng))
def skew(rng, n, shape):
    ex = rng.choice(np.array([1, 3, 6], np.float32), (N, 8, 1, 1))
    return np.minimum((n * rng.random(shape, dtype=np.float32) ** ex).astype(np.int64), n - 1)
def setup_inputs_spread(rng):
    x = np.minimum((16 * rng.random((N, 8, 1, WX), dtype=np.float32) * rng.random((N, 8, 16, WX), dtype=np.float32)).astype(np.int64), 15)
    x = np.where(rng.random((N, 8, 1, WX)) < 0.5, 15 - x, x)
    g = np.minimum((16 * rng.random((N, 8, 1, I)) * rng.random((N, 8, 16, I))).astype(np.int64), 15)
    return pack(x, g, skew(rng, W, (N, 8, 16, W)) + W * skew(rng, WX, (N, 8, 16, W)), skew(rng, W, (N, 8, 16, I)), skew(rng, WX, (N, 8, 16, I)))
def atends(rng, hi, shape, share):
    u = rng.random(shape)
    return np.where(u < 0.5 * share, 0, np.where(u < share, hi, rng.integers(0, hi + 1, shape)))
def kinds(rng, n):
    m = rng.random((N, 8, 1, n)); e = rng.integers(0, 2, (N, 8, 16, n))
    return 15 * np.where(m < 0.25, 0, np.where(m < 0.5, 1, e))
def setup_inputs_ends(rng):
    x = kinds(rng, WX); g = kinds(rng, I); big = W * WX - 1
    u = rng.random((N, 8, 16, W)); two = rng.integers(0, 2, u.shape)
    rel = np.where(u < 0.35, 0, np.where(u < 0.7, big, np.where(u < 0.85, np.where(two == 1, W - 1, W * (WX - 1)), rng.integers(0, W * WX, u.shape))))
    nam = atends(rng, W - 1, (N, 8, 16, I), 0.75); grd = atends(rng, WX - 1, (N, 8, 16, I), 0.75)
    for c in (0, WX - 1):
        x[:, :, :, c] = 15 * rng.integers(0, 2, (N, 8, 16)); x[0, :, :, c] = 0; x[1, :, :, c] = 15; x[N - 1, :, :, c] = 15
    for q in (0, 1, N - 1): grd[q] = (WX - 1) * rng.integers(0, 2, (8, 16, I))
    for q in (1, N - 1):
        turn = (np.arange(16)[None, :, None] + rng.integers(0, 16, (8, 1, I))) & 15
        g[q] = np.where(turn < 8, 0, g[q]); g[q, 7, :, I - 1] = 0; g[q, 0, :, 0] = 0; g[q, 3, :8, I - 1] = 0; g[q, 3, 8:, I - 1] = 15
    for q in range(N):
        if 1 < q < N - 1 or q == 0: g[q, :, :, 0] = 15; g[q, :, :, I - 1] = 15; g[q, :, :, 1] = 0; g[q, :, :, I - 2] = 0
    x[1, 7, :, WX // 2] = 0; grd[1, 7, 15, I - 1] = WX // 2
    for q in range(N):
        rel[q, 7, 15, W - 1] = big; rel[q, 0, 0, 0] = big; rel[q, 7, 15, 0] = 0; nam[q, 0, 0, 0] = 0; nam[q, 7, 15, I - 1] = W - 1; nam[q, 7, 0, I - 1] = W - 1
    return pack(x, g, rel, nam, grd)
def setup_inputs_corners(rng):
    x, g, rel, nam, grd = parts(rng)
    g = rng.integers(0, 15 - GAP, (N, 8, 16, I)); ones = np.arange(16)[:, None]
    ty = np.array([(16, 0), (0, 16), (0, 0), (DR, 16 - DR), (DR - 1, 17 - DR), (0, IR - 1), (0, IR), (DR + 1, 0), (16 - IR, IR), (17 - IR, IR - 1), (DR, 0), (DR - 1, 0)])
    c = np.arange(WX) & (B - 1); which = np.where(c < 8, c, rng.integers(0, 12, (N, 8, WX)))
    over = ty[which, 0][:, :, None, :]; under = ty[which, 1][:, :, None, :]
    role = (ones * (2 * rng.integers(0, 8, (N, 8, 1, WX)) + 1) + rng.integers(0, 16, (N, 8, 1, WX))) & 15
    gg = np.repeat(g, B, axis=3); coin = rng.random(gg.shape) < 0.5
    v = np.where(role < over, np.where(coin, gg + GAP + 1, 15), np.where(role >= 16 - under, np.where(coin, gg, 0), np.where(coin, gg + 1, gg + GAP)))
    ca = (np.arange(I) + rng.integers(0, 10, (N, 8, 1, 1))) % 10; r = rng.integers(0, B, (N, 8, 16, I)); two = rng.integers(0, 2, (N, 8, 16, I))
    cs = np.where(ca == 1, 0, np.where(ca == 2, 1, np.where(ca == 3, 2, r)))
    cs = np.where(ca == 4, np.where(ones == 15, 2, 0), np.where(ca == 5, np.where(ones == 0, 2, two), cs))
    cs = np.where(ca == 6, 3 + (r & 3), np.where(ca == 7, two, np.where(ca == 8, np.where(ones == 15, 0, 1), cs)))
    col = B * np.arange(I) + cs
    for q in range(N):
        for w in range(8):
            o = rng.permutation(WX); x[q, w][:, o] = v[q, w]; grd[q, w] = o[col[q, w]]
    g = np.where(ca == 9, 15, g)
    l = np.arange(W); m = rng.integers(0, 5, rel.shape)
    rel = np.where(m == 0, l + W * np.minimum(l, WX - 1), np.where(m == 1, l + W * (rel >> SH), np.where(m == 2, (W - 1) * rng.integers(0, 2, rel.shape) + W * (WX - 1) * rng.integers(0, 2, rel.shape), rel)))
    nam = np.where(rng.random(nam.shape) < 0.3, (W - 1) * rng.integers(0, 2, nam.shape), nam)
    return pack(x, g, rel, nam, grd)
def setup_inputs_alike(rng):
    x, g, rel, nam, grd = parts(rng)
    grd[:, ::2] = rng.choice(np.array([0, WX - 1, WX // 2, 3]), (N, 4, 16, I)); grd[:, 1] = np.repeat(grd[:, 1, :1], 16, axis=1)
    nam[:, 2] = rng.choice(np.array([0, W - 1]), (N, 16, I)); nam[:, 3] = np.repeat(nam[:, 3, :1], 16, axis=1)
    rel[:, 5] = rng.choice(rng.integers(0, W * WX, 6), (N, 16, W)); rel[:, 7] = np.repeat(rel[:, 7, :1], 16, axis=1)
    x[:, 4] = 4 + GAP + rng.integers(0, 2, (N, 16, WX)); g[:, 4] = rng.choice(np.array([4, 4 + GAP]), (N, 16, I))
    x[N - 1, 4] = rng.integers(5, 5 + GAP, (16, WX)); g[N - 1, 4] = 4
    for q in range(N):
        c = int(rng.choice(np.array([0, WX - 1, WX // 2, 3]))); grd[q, 6] = c; x[q, 6, :, c] = rng.permutation(16)
        grd[q, 7] = rng.permutation(np.arange(16 * I) % WX).reshape(16, I)
    return pack(x, g, rel, nam, grd)
def check_inputs(d):
    bad = []
    for k, hi in (("xc", 15), ("rel", W * WX - 1), ("nam", W - 1), ("grd", WX - 1), ("lim", 15)):
        v = np.asarray(d[k]).astype(np.float64)
        if not (np.min(v) >= 0 and np.max(v) <= hi): bad.append("range of " + k)
        elif np.any(v != np.floor(v)): bad.append("whole numbers of " + k)
    return bad
def reference(xc, rel, nam, grd, lim):
    x = xc.astype(np.float32).astype(np.int32).reshape(N, 8, 16, WX); g = lim.astype(np.float32).astype(np.int32).reshape(N, 8, 16, I)
    tab = rel.reshape(N, 8, 16, W); a = nam.astype(np.int32).reshape(N, 8, 16, I); b = grd.astype(np.int32).reshape(N, 8, 16, I)
    deaths = np.zeros(N, np.int64); wt = (2 * np.arange(16) + 1)[None, :, None]
    for t in range(RO):
        for q in range(N):
            v = np.take_along_axis(x[q], b[q].reshape(8, 1, 16 * I), 2).reshape(8, 16, 16, I)
            gq = g[q][:, :, None, :]
            over = np.sum(v > gq + GAP, axis=1); under = np.sum(v <= gq, axis=1)
            dead = over >= DR + (deaths[q] & 1); imp = ~dead & (under >= IR); und = ~dead & ~imp
            some = np.any(und, axis=1); s = np.argmax(und, axis=1)
            z = np.where(dead, np.take_along_axis(a[q], s[:, None, :], 1), a[q])
            new = np.take_along_axis(tab[q], z, 2)
            vs = np.take_along_axis(v, s[:, None, None, :], 2)[:, :, 0]
            g[q] = np.where(some[:, None, :], np.maximum(g[q], vs), g[q])
            a[q] = np.where(und, a[q], new & (W - 1)); b[q] = np.where(und, b[q], new >> SH)
            deaths[q] = np.sum(dead)
        sent = np.array(g)
        for q in range(N):
            h = sent[(q - 1 - t % (N - 1)) % N]
            if t < RO - 1:
                place = B * np.arange(I) + (np.sum(wt * h, axis=1) & (B - 1))
                place = np.repeat(place[:, None, :], 16, axis=1)
                np.put_along_axis(x[q], place, (np.take_along_axis(x[q], place, 2) + h) >> 1, 2)
            g[q] = np.minimum(sent[q], h + 2)
    return {"yn": a.reshape(N, 128, I).astype(np.float32), "yg": b.reshape(N, 128, I).astype(np.float32), "yl": g.reshape(N, 128, I).astype(np.float32).astype(BF)}

import numpy as np
from concourse.mybir import dt, AluOpType, AxisListType, ActivationFunctionType

I = 224
WX = 1792
W = 2048
RO = 4
CH = [(0, 80), (80, 160), (160, 224)]
DG = [(0, 96), (96, 160), (160, 224)]

SB = "sbuf"
BF, F32, I32, U16 = "bfloat16", "float32", "int32", "uint16"
SCRATCH = {
    "x": (SB, [128, WX], BF), "lim0": (SB, [128, I], BF), "grd0": (SB, [128, I], I32), "nam0": (SB, [128, I], I32),
    "rel0": (SB, [128, W], I32), "mf": (SB, [128, W], F32),
    "p0": (SB, [128, W], BF), "p1": (SB, [128, W], BF), "p2": (SB, [128, W], BF), "i1": (SB, [128, W], I32), "i2": (SB, [128, W], I32),
    "wt": (SB, [128, 4 * W], BF),
    "ku": (SB, [128, I], U16), "lu": (SB, [128, I], U16), "pn": (SB, [128, I], I32), "ki": (SB, [128, I], I32), "li": (SB, [128, I], I32),
    "d": (SB, [128, 11264], BF), "ov": (SB, [128, 16 * I], BF), "un": (SB, [128, 16 * I], BF), "grep": (SB, [128, 16 * I], BF),
    "il": (SB, [128, I], F32), "gl": (SB, [128, I], U16), "nf": (SB, [128, 16 * I], F32), "nb": (SB, [128, 16 * I], BF),
    "gm": (SB, [128, I], BF), "dead": (SB, [128, I], BF), "imp": (SB, [128, I], BF), "hot": (SB, [128, I], "float16"), "hol": (SB, [128, I], BF),
    "oln": (SB, [128, I], "float16"), "slu": (SB, [128, 14], U16), "llu": (SB, [128, 14], U16),
    "ya": (SB, [128, I], BF), "w1": (SB, [128, I], F32), "w3": (SB, [128, I], F32),
    "qi": (SB, [128, 14], I32), "qj": (SB, [128, 14], I32), "qk": (SB, [128, 14], I32), "cu": (SB, [128, 14], U16), "bl": (SB, [128, I], BF),
    "cnt": (SB, [128, 1], F32), "pi": (SB, [128, 1], I32), "pj": (SB, [128, 1], I32), "thd": (SB, [128, 1], F32),
    "thb": (SB, [128, 1], F32), "thl": (SB, [128, 1], F32), "kz": (SB, [128, 1], F32), "seg": (SB, [128, 1], F32),
    "kcol": (SB, [128, 1], F32), "kc16": (SB, [128, 1], F32), "kc8": (SB, [128, 1], F32), "km": (SB, [128, 1], F32), "wcol": (SB, [128, 1], F32),
    "ones": (SB, [128, I], BF), "half": (SB, [128, I], BF), "onef": (SB, [128, 128], F32),
    "tri": (SB, [128, 128], BF), "trz": (SB, [128, 128], BF), "idb": (SB, [128, 128], BF), "idf": (SB, [128, 128], "float16"), "nid": (SB, [128, 128], BF),
    "nbig": (SB, [128, 128], BF),
    "g8": (SB, [128, 8], BF), "i8": (SB, [128, 8], F32), "k8": (SB, [128, 8], F32), "z32": (SB, [128, 32], F32), "s32": (SB, [128, 32], F32),
    "q0": (SB, [128, 1], F32), "q1": (SB, [128, 1], F32), "q2": (SB, [128, 1], F32), "q3": (SB, [128, 1], F32),
    "ib": (SB, [128, 15], F32), "iq": (SB, [128, 14], F32), "bs": (SB, [128, 15], "float16"), "bq": (SB, [128, 14], I32),
    "cc": (SB, [128, 2048], BF), "cs": (SB, [128, 2048], "float16"), "cw": (SB, [128, 2048], BF), "cf": (SB, [128, 2048], "float16"),
    "pp": (SB, [128, 2048], BF), "ee": (SB, [128, 2048], F32),
    "on": (SB, [128, I], F32), "og": (SB, [128, I], F32), "ol": (SB, [128, I], BF),
}
for _t in range(RO):
    SCRATCH["gs%d" % _t] = (SB, [128, I], BF)
    SCRATCH["h%d" % _t] = (SB, [128, I], BF)
PSUM = ("po", "pu", "pb", "pl", "pm", "pd", "px", "pg")
for _b in PSUM:
    SCRATCH[_b] = ("psum", [128, 512], F32)

SEMAPHORES = ["cv", "ca", "ct", "cg", "sent", "d_x", "d_lim", "d_grd", "d_nam", "d_rel", "d_on", "d_og", "d_ol", "d_wt"]
SEMAPHORES += ["arr%d" % _t for _t in range(RO)]


def rank_program(g, core, T, topo):
    rank = T.rank_of(core)
    if rank is None:
        return
    A, F, X = AluOpType, ActivationFunctionType, AxisListType.X
    queue = {"v": g.vector, "a": g.scalar, "t": g.tensor, "g": g, "s": g.sync}
    count = {q: 0 for q in queue}
    known = {q: {} for q in queue}
    wrote, seen = {}, {}
    dcount = {}

    def need(q, rec):
        sem, val, snap = rec[1], rec[2], rec[3]
        if known[q].get(sem, 0) < val:
            queue[q].wait_ge(T.sem[sem], val)
            known[q][sem] = val
            for s in snap:
                known[q][s] = max(known[q].get(s, 0), snap[s])

    def waits(q, reads, writes):
        recs = []
        for k in reads:
            if k in wrote:
                recs.append(wrote[k])
            if k in PSUM:
                recs += [r for r in seen.get(k, {}).values() if r[0] != q]
        for k in writes:
            if k in wrote and (wrote[k][0] != q or (q != "t" and k != "cc")):
                recs.append(wrote[k])
            recs += [r for r in seen.get(k, {}).values() if r[0] != q]
        for r in sorted(recs, key=lambda r: -r[2]):
            need(q, r)

    def note(rec, reads, writes):
        for k in reads:
            seen.setdefault(k, {})[rec[0]] = rec
        for k in writes:
            wrote[k] = rec
            seen[k] = {}

    def op(q, reads, writes, fn):
        waits(q, reads, writes)
        ins = fn(queue[q])
        count[q] += 1
        ins.then_inc(T.sem["c" + q], 1)
        snap = dict(known[q])
        snap["c" + q] = count[q]
        note((q, "c" + q, count[q], snap), reads, writes)

    def load(q, sem, out, in_, reads, writes):
        waits(q, reads, writes)
        queue[q].dma_start(out, in_).then_inc(T.sem[sem], 16)
        dcount[sem] = dcount.get(sem, 0) + 16
        snap = dict(known[q])
        snap[sem] = dcount[sem]
        note(("dma" + sem, sem, dcount[sem], snap), reads, writes)

    def copy(out, okey, in_, ikeys):
        op("v", ikeys, [okey], lambda e: e.tensor_copy(out, in_))

    def ts(out, okey, in_, ikeys, s1, s2, op0, op1=None):
        if op1 is None:
            op("v", ikeys, [okey], lambda e: e.tensor_scalar(out, in_, s1, None, op0))
        else:
            op("v", ikeys, [okey], lambda e: e.tensor_scalar(out, in_, s1, s2, op0, op1))

    def tt(out, okey, a, b, ikeys, o):
        op("v", ikeys, [okey], lambda e: e.tensor_tensor(out, a, b, o))

    def act(out, okey, in_, ikeys, f=F.Copy, **kw):
        op("a", ikeys, [okey], lambda e: e.activation(out, in_, f, **kw))

    def mm(bank, a, b, lhs, lkey, rhs, rkey, start, stop):
        op("t", [lkey, rkey], [bank], lambda e: e.matmul(T[bank][:, a:b], lhs, rhs, start, stop))

    def memset(name, val, key=None):
        op("v", [], [key or name], lambda e: e.memset(T[name][:], val))

    def select(name, src, pattern, cmp, fill, base, mult):
        op("g", [src], [name], lambda e: e.affine_select(T[name][:], T[src][:, 0:T[name].shape[1]], pattern, cmp, fill, base, mult))

    def iota(name, pattern, mult):
        op("g", [], [name], lambda e: e.iota(T[name][:], pattern, 0, mult, allow_small_or_imprecise_dtypes=True))

    def block(name):
        select(name, name, [[-16, 8], [0, 16]], A.is_ge, 0.0, 0, 1)
        select(name, name, [[16, 8], [0, 16]], A.is_ge, 0.0, 15, -1)

    def part(name, k):
        return T[name][:, 128 * k:128 * k + 128]

    def repeat(c, src, bias):
        a, b = CH[c]
        act(T.grep[:, 16 * a:16 * b], "grep%d" % c, T[src][:, 0:I].indirect(T.gl[:, a:b]), [src, "gl"], bias=bias)

    def judge(c):
        a, b = CH[c]
        tt(T.d[:, 4096 * c:4096 * c + 16 * (b - a)], "d%d" % c, T.x[:, 0:WX].indirect(T.ku[:, a:b]), T.grep[:, 16 * a:16 * b],
           ["x", "ku", "grep%d" % c], A.subtract)

    def under(c):
        a, b = CH[c]
        ts(T.un[:, 16 * a:16 * b], "un%d" % c, T.d[:, 4096 * c:4096 * c + 16 * (b - a)], ["d%d" % c], 0.5, None, A.is_lt)

    def over(c):
        a, b = CH[c]
        act(T.ov[:, 16 * a:16 * b], "ov%d" % c, T.d[:, 4096 * c:4096 * c + 16 * (b - a)], ["d%d" % c], F.Sign, bias=-4.5)

    def tally(c, nm):
        a, b = CH[c]
        for k in range(16):
            mm("pu" if nm == "un" else "po", a, b, part("cc", k), "cc", T[nm][:, 16 * a + k:16 * b:16], "%s%d" % (nm, c), k == 0, k == 15)

    def fetch(j):
        a, b = DG[j]
        act(T.nb[:, 16 * a:16 * b], "nb%d" % j, T.wt[:, 0:4 * W].indirect(T.lu[:, a:b]), ["wt", "lu"])

    def pick(j):
        a, b = DG[j]
        mm("pd", a, b, T.nbig[:], "nbig", T.ones[:, a:b], "ones", True, False)
        for k in range(16):
            mm("pd", a, b, part("pp", k), "pp", T.nb[:, 16 * a + k:16 * b:16], "nb%d" % j, False, k == 15)

    def pieces(u):
        for q in range(4):
            for v in ((u, 3) if u == 2 else (u,)):
                load("s", "d_wt", T.wt[v::4, W * q:W * q + W], T["p%d" % u][q::4, :], ["p%d" % u], ["wt%d%d" % (v, q)])
                wrote["wt"] = wrote["wt%d%d" % (v, q)]

    alld = ["d%d" % c for c in range(len(CH))] + ["dz%d" % c for c in range(len(CH))]
    late = []

    load("s", "d_grd", T.grd0[:], T.grd[:], [], ["grd0"])
    load("a", "d_lim", T.lim0[:], T.lim[:], [], ["lim0"])
    load("s", "d_x", T.x[:], T.xc[:], [], ["x"])
    load("s", "d_nam", T.nam0[:], T.nam[:], [], ["nam0"])
    load("s", "d_rel", T.rel0[:], T.rel[:], [], ["rel0"])

    memset("ones", 1.0)
    memset("tri", 2.0)
    memset("trz", 1.0)
    memset("z32", 0.0)
    memset("s32", 0.0)
    memset("thd", -5.0)
    iota("il", [[1, I]], 0)
    copy(T.gl[:], "gl", T.il[:], ["il"])
    memset("cc", 0.0, "zero")
    iota("i8", [[-16, 8]], 1)
    select("g8", "ones", [[-16, 8]], A.is_ge, 0.0, 0, 1)
    select("g8", "g8", [[16, 8]], A.is_ge, 0.0, 15, -1)
    iota("ib", [[4096, 3], [256, 5]], 0)
    iota("iq", [[128, 14]], 0)
    select("idb", "ones", [[-1, 128]], A.is_equal, 0.0, 0, 1)
    select("tri", "tri", [[1, 128]], A.is_gt, 0.0, 0, -1)
    select("tri", "tri", [[1, 128]], A.not_equal, -1.0, 0, -1)
    block("tri")
    select("trz", "trz", [[1, 128]], A.not_equal, -15.0, 0, -1)
    select("trz", "trz", [[0, 8], [1, 16]], A.is_equal, 0.0, 0, 0)
    block("trz")
    for u, w in enumerate((32768.0, 128.0, 1.0)):
        select("z32", "z32", [[-4, 4], [-16, 8]], A.not_equal, w, -u, 1)
    for u in (1, 2, 3):
        select("s32", "s32", [[-4, 4], [-16, 8]], A.not_equal, float(W * u), -u, 1)

    for t in range(RO):
        last = t == RO - 1
        h = "h%d" % (t - 1)
        if t == 0:
            copy(T.ku[:], "ku", T.grd0[:], ["grd0"])
            for k in range(16):
                copy(T.cc[:, 129 * k:128 * k + 128:16], "cc", T.g8[:], ["g8", "zero"])
            for c in range(len(CH)):
                repeat(c, "lim0", 0.4375)
            act(T.pg[:, 0:I], "pg", T.lim0[:], ["lim0"], bias=-192.0)
        else:
            tt(T.gm[:], "gm", T[h][:], T.pg[:, 256:256 + I], ["pg", h], A.min)
            for r in range(16):
                mm("pl", 32, 46, part("cw", r), "cw", T[h][:, r::16], h, r == 0, r == 15)
            for c in range(len(CH)):
                repeat(c, "gm", 2.4375)
            act(T.pg[:, 0:I], "pg", T.gm[:], ["gm"], bias=-190.0)
            copy(T.qi[:], "qi", T.pl[:, 32:46], ["pl"])
            ts(T.qj[:], "qj", T.qi[:], ["qi"], 7, None, A.bitwise_and)
            tt(T.qk[:], "qk", T.qj[:], T.bq[:], ["qj", "bq"], A.add)
            copy(T.cu[:], "cu", T.qk[:], ["qk"])
            tt(T.bl[:], "bl", T.x[:, 0:WX].indirect(T.cu[:]), T[h][:], ["x", "cu", h], A.add)
            tt(T.x[:, 0:WX].indirect(T.cu[:]), "x", T.bl[:], T.half[:], ["bl", "cu", "half"], A.mult)
        judge(0)
        over(0)
        under(0)
        if t == 0:
            tt(T.k8[:], "k8", T.i8[:], T.g8[:], ["i8", "g8"], A.mult)
            op("v", ["k8"], ["kcol"], lambda e: e.tensor_reduce(T.kcol[:], T.k8[:], X, A.add))
            op("v", ["s32"], ["seg"], lambda e: e.tensor_reduce(T.seg[:], T.s32[:], X, A.add))
            ts(T.lu[:], "lu", T.nam0[:], ["nam0", "seg"], T.seg[:], None, A.add)
            ts(T.kz[:], "kz", T.kcol[:], ["kcol"], 0.5, None, A.is_lt)
            ts(T.thb[:], "thb", T.kcol[:], ["kcol"], 2.0, -0.5, A.mult, A.add)
            ts(T.kc16[:], "kc16", T.kcol[:], ["kcol"], 16.0, 2048.0, A.mult, A.add)
            ts(T.kc8[:], "kc8", T.kcol[:], ["kcol"], 8.0, None, A.mult)
            ts(T.km[:], "km", T.kcol[:], ["kcol"], -2048.0, None, A.add)
            ts(T.wcol[:], "wcol", T.kcol[:], ["kcol"], 2.0, 1.0, A.mult, A.add)
            tt(T.thl[:], "thl", T.thb[:], T.kz[:], ["thb", "kz"], A.subtract)
            ts(T.bs[:], "bs", T.ib[:], ["ib", "kc16"], T.kc16[:], None, A.add)
            ts(T.bq[:], "bq", T.iq[:], ["iq", "kc8"], T.kc8[:], None, A.add)
            for q in range(4):
                op("v", ["z32"], ["q%d" % q], lambda e, q=q: e.tensor_reduce(T["q%d" % q][:], T.z32[:, 8 * q:8 * q + 8], X, A.add))
        for fn in late:
            fn()
        late = []
        for c in (1, 2):
            tally(c - 1, "un")
            tally(c - 1, "ov")
            judge(c)
            over(c)
            if c == 1:
                under(1)
                if t == 0:
                    for q in range(4):
                        act(T.pp[:, 512 * q:512 * q + 512], "pp", T.cc[:, 512 * q:512 * q + 512], ["cc", "q%d" % q], scale=T["q%d" % q][:])
                    act(T.cw[:], "cw", T.cc[:], ["cc", "wcol"], scale=T.wcol[:])
                    ts(T.p0[:], "p0", T.rel0[:], ["rel0"], 2.0 ** -15, 128.5 + 2.0 ** -16, A.mult, A.add)
                    pieces(0)
                    ts(T.i1[:], "i1", T.rel0[:], ["rel0"], 7, 255, A.arith_shift_right, A.bitwise_and)
                    ts(T.i2[:], "i2", T.rel0[:], ["rel0"], 127, None, A.bitwise_and)
                    copy(T.p1[:], "p1", T.i1[:], ["i1"])
                    pieces(1)
                    copy(T.p2[:], "p2", T.i2[:], ["i2"])
                    pieces(2)
        under(2)
        if t == 0:
            for c, (a, b) in enumerate(CH):
                lo = 4096 * c + 2048
                op("v", [], ["dz%d" % c], lambda e, lo=lo, n=16 * (b - a): e.memset(T.d[:, lo:lo + n], 0.0))
            copy(T.idf[:], "idf", T.idb[:], ["idb"])
            tt(T.trz[:], "trz", T.trz[:], T.tri[:], ["trz", "tri"], A.add)
            ts(T.cs[:], "cs", T.cc[:], ["cc", "km"], T.km[:], None, A.mult)
            copy(T.cf[:], "cf", T.cc[:], ["cc"])
        tally(2, "un")
        tally(2, "ov")
        for j in range(len(DG)):
            fetch(j)
        ts(T.imp[:], "imp", T.pu[:, 0:I], ["pu"], 11.5, None, A.is_gt)
        ts(T.dead[:], "dead", T.po[:, 0:I], ["po", "thd"], T.thd[:], None, A.is_gt)
        mm("pb", 0, I, T.trz[:], "trz", T.imp[:], "imp", True, False)
        mm("pb", 0, I, T.trz[:], "trz", T.dead[:], "dead", False, True)
        mm("pl", 0, 14, T.idf[:], "idf", T.bs[:, 0:14], "bs", True, False)
        ts(T.hot[:], "hot", T.pb[:, 0:I], ["pb", "thb"], T.thb[:], None, A.is_gt)
        for r in range(16):
            mm("pl", 0, 14, part("cs", r), "cs", T.hot[:, r::16], "hot", False, r == 15)
        ts(T.hol[:], "hol", T.pb[:, 0:I], ["pb", "thl"], T.thl[:], None, A.is_gt)
        names = "nam0" if t == 0 else "li"
        tt(T.oln[:], "oln", T.hol[:], T[names][:], ["hol", names], A.mult)
        copy(T.slu[:], "slu", T.pl[:, 0:14], ["pl"])
        ts(T.ya[:], "ya", T.d[:, 0:11264].indirect(T.slu[:]), alld + ["slu"], -0.4375, 192.0, A.max, A.add)
        gs = "gs%d" % t
        tt(T[gs][:], gs, T.ya[:], T.pg[:, 0:I], ["ya", "pg"], A.add)
        dst = T.cores[(rank + 1 + t % 7) % 8]
        src = T.cores[(rank - 1 - t % 7) % 8]
        eng = topo.engines(core, dst)[:8]
        rid, pid = topo.addr(dst, core)
        waits("g", [gs], [])
        g.remote_dma(T["h%d" % t][:], T[gs][:], T.sem["arr%d" % t], T.sem.sent, pid, rid, sum(1 << e for e in eng))
        wrote["h%d" % t] = ("remote", "arr%d" % t, len(topo.engines(src, core)[:8]), {})
        ts(T.pg[:, 256:256 + I], "pg", T[gs][:], [gs], -2.0, None, A.add)
        if t == 0:
            ts(T.nid[:], "nid", T.idb[:], ["idb"], -1.0, None, A.mult)
            ts(T.ki[:], "ki", T.grd0[:], ["grd0"], 2048.0, None, A.mult)
            tt(T.pn[:], "pn", T.ki[:], T.nam0[:], ["ki", "nam0"], A.add)
            memset("onef", 1.0)
            memset("half", 0.5)
            ts(T.nbig[:], "nbig", T.idb[:], ["idb"], -129.0 * 32768.0, None, A.mult)
        for r in range(16):
            mm("pl", 64, 78, part("cf", r), "cf", T.oln[:, r::16], "oln", r == 0, r == 15)
        mm("px", 0, I, T.idb[:], "idb", T.ones[:], "ones", True, False)
        mm("px", 0, I, T.nid[:], "nid", T.dead[:], "dead", False, False)
        mm("px", 0, I, T.nid[:], "nid", T.imp[:], "imp", False, True)
        for j in range(len(DG)):
            pick(j)
        copy(T.llu[:], "llu", T.pl[:, 64:78], ["pl"])
        tt(T.px[:, 0:I], "px", T.pn[:], T.px[:, 0:I], ["pn", "px"], A.mult)
        tt(T.w1[:], "w1", T.rel0[:, 0:W].indirect(T.llu[:]), T.dead[:], ["rel0", "llu", "dead"], A.mult)
        tt(T.w3[:], "w3", T.w1[:], T.px[:, 0:I], ["w1", "px"], A.add)
        tt(T.pd[:, 0:I], "pd", T.imp[:], T.pd[:, 0:I], ["imp", "pd"], A.mult)
        tt(T.pn[:], "pn", T.w3[:], T.pd[:, 0:I], ["w3", "pd"], A.add)
        ts(T.ki[:], "ki", T.pn[:], ["pn"], 11, None, A.arith_shift_right)
        if not last:
            copy(T.ku[:], "ku", T.ki[:], ["ki"])
            late = [
                lambda: op("v", ["dead"], ["cnt"], lambda e: e.tensor_reduce(T.cnt[:], T.dead[:], X, A.add)),
                lambda: ts(T.li[:], "li", T.pn[:], ["pn"], 2047, None, A.bitwise_and),
                lambda: mm("pm", 0, 1, T.onef[:], "onef", T.cnt[:], "cnt", True, True),
                lambda: ts(T.lu[:], "lu", T.li[:], ["li", "seg"], T.seg[:], None, A.add),
                lambda: copy(T.pi[:], "pi", T.pm[:, 0:1], ["pm"]),
                lambda: ts(T.pj[:], "pj", T.pi[:], ["pi"], 1, None, A.bitwise_and),
                lambda: ts(T.thd[:], "thd", T.pj[:], ["pj"], 2.0, -5.0, A.mult, A.add)]
        else:
            copy(T.og[:], "og", T.ki[:], ["ki"])
            load("s", "d_og", T.yg[:], T.og[:], ["og"], ["yg"])
            ts(T.li[:], "li", T.pn[:], ["pn"], 2047, None, A.bitwise_and)
            copy(T.on[:], "on", T.li[:], ["li"])
            load("s", "d_on", T.yn[:], T.on[:], ["on"], ["yn"])
            h = "h%d" % t
            tt(T.gm[:], "gm", T[h][:], T.pg[:, 256:256 + I], ["pg", h], A.min)
            ts(T.ol[:], "ol", T.gm[:], ["gm"], 2.0, None, A.add)
            load("a", "d_ol", T.yl[:], T.ol[:], ["ol"], ["yl"])
    g.wait_ge(T.sem.sent, sum(len(topo.engines(core, T.cores[(rank + 1 + t % 7) % 8])[:8]) for t in range(RO)))
    for q in ("v", "a", "t", "g"):
        if known["g"].get("c" + q, 0) < count[q]:
            g.wait_ge(T.sem["c" + q], count[q])
    for s in ("d_on", "d_og", "d_ol"):
        g.wait_ge(T.sem[s], 16)
